import numpy as np
import ml_dtypes


def mxq(x, axis, fmt="e4m3"):
    dtype, down = {"e4m3": (ml_dtypes.float8_e4m3fn, 7), "e5m2": (ml_dtypes.float8_e5m2, 14)}[fmt]
    v = np.moveaxis(np.asarray(x, np.float32).astype(ml_dtypes.bfloat16).astype(np.float64), axis, -1)
    blocks = v.reshape(v.shape[:-1] + (-1, 32))
    amax = np.abs(blocks).max(-1, keepdims=True)
    byte = np.maximum(np.where(amax > 0, np.frexp(amax)[1] - 1 + 127, 0) - down, 1)
    scale = np.exp2(byte - 127.0)
    codes = (blocks / scale).astype(np.float32).astype(dtype).astype(np.float64)
    return np.moveaxis((codes * scale).reshape(v.shape), -1, axis)


WIDE = False


def mx_kscale(k):
    if not WIDE:
        return np.ones(k)
    levels = np.array([10, -10, 5, -5, 0])
    if k % 512:
        return np.exp2(np.random.permutation(np.resize(levels, k // 32))).repeat(32)
    a = np.empty((k // 512, 16))
    for p in range(k // 512):
        a[p, :8] = np.random.permutation(np.resize(levels, 8))
        for g in range(8):
            far = levels[np.abs(levels - a[p, g]) >= 10]
            a[p, g + 8] = far[np.random.randint(len(far))]
    return np.exp2(a.ravel()).repeat(32)


def f64(x):
    return np.asarray(x).astype(np.float64)


def striped(idx):
    return np.tile(np.asarray(idx).reshape(-1, 16).T, (8, 1)).astype(np.uint16)


def unstriped(offs):
    return offs[:16].T.reshape(-1).astype(np.int64)


E2M1 = np.array([0.0, 0.5, 1.0, 1.5, 2.0, 3.0, 4.0, 6.0, -0.0, -0.5, -1.0, -1.5, -2.0, -3.0, -4.0, -6.0])


def pack_weight(w, fmt):
    k, n = w.shape
    w = f64(np.asarray(w, np.float32).astype(ml_dtypes.bfloat16)).reshape(k // 32, 32, n)
    amax = np.abs(w).max(1)
    if fmt == "e4m3":
        byte = np.frexp(amax)[1] - 1 + 127 - 7
    else:
        mant, ex = np.frexp(amax / 6.0)
        byte = np.where(mant > 0.5, ex, ex - 1) + 127
    byte = np.clip(np.where(amax > 0, byte, 1), 1, 254)
    scaled = (w * np.exp2(127.0 - byte)[:, None, :]).reshape(k, n).astype(np.float32)
    by_word = np.ascontiguousarray(scaled.reshape(k // 512, 128, 4, n).transpose(0, 1, 3, 2))
    if fmt == "e4m3":
        words = by_word.astype(ml_dtypes.float8_e4m3fn).view(np.uint8)
    else:
        c = by_word.astype(ml_dtypes.float4_e2m1fn).view(np.uint8) & 0xF
        words = (c[..., 0::2] | (c[..., 1::2] << 4)).reshape(k // 512, 128, 2 * n)
    return np.ascontiguousarray(words), np.ascontiguousarray(byte.astype(np.uint8).reshape(k // 512, 16, n))


def unpack_weight(words, scales, fmt):
    g, _, n = scales.shape
    words = np.ascontiguousarray(words).reshape(g, 128, n, -1)
    if fmt == "e4m3":
        vals = words.view(ml_dtypes.float8_e4m3fn).astype(np.float64)
    else:
        nib = np.empty((g, 128, n, 4), np.uint8)
        nib[..., 0::2] = words & 0xF
        nib[..., 1::2] = words >> 4
        vals = E2M1[nib]
    vals = vals * np.repeat(np.exp2(scales.astype(np.float64) - 127.0), 8, axis=1)[..., None]
    return vals.transpose(0, 1, 3, 2).reshape(g * 512, n)


def bf(x):
    return np.asarray(x, np.float32).astype(ml_dtypes.bfloat16)


def planes(Y):
    r, m = Y.shape
    b = f64(bf(Y)).reshape(r // 32, 32, m)
    amax = np.abs(b).max(1)
    byte = np.clip(np.where(amax > 0, np.frexp(amax)[1] - 1 + 127 - 7, 1), 1, 254)
    codes = (b * np.exp2(127.0 - byte)[:, None, :]).reshape(r, m).astype(np.float32).astype(ml_dtypes.float8_e4m3fn).view(np.uint8)
    words = codes.reshape(r // 512, 128, 4, m).transpose(0, 1, 3, 2)
    return np.ascontiguousarray(words), np.ascontiguousarray(byte.astype(np.uint8).reshape(r // 512, 16, m))


K, T, C, J, N = 512, 512, 2048, 512, 512


def setup_inputs():
    n = np.random.standard_normal
    idx = np.random.permutation(C)[:J]
    fk = mx_kscale(K)
    fj = mx_kscale(J)
    xtp = pack_weight(n((K, T)) * 0.3 / fk[:, None], "e2m1")
    wcp = pack_weight(n((K, C)) * 1 / np.sqrt(K) * fk[:, None], "e4m3")
    wop = pack_weight(n((J, N)) * 1 / np.sqrt(J) / fj[:, None], "e2m1")
    wsp = pack_weight(n((K, N)) * 1 / np.sqrt(K) * fk[:, None], "e4m3")
    return {
        "xt_words": xtp[0],
        "xt_scales": xtp[1],
        "wc_words": wcp[0],
        "wc_scales": wcp[1],
        "fj": (np.random.uniform(64.0, 128.0, (J, 1)) * fj[:, None]).astype(np.float32),
        "wo_words": wop[0],
        "wo_scales": wop[1],
        "ws_words": wsp[0],
        "ws_scales": wsp[1],
        "offs": striped(idx),
    }


def reference(xt_words, xt_scales, wc_words, wc_scales, fj, wo_words, wo_scales, ws_words, ws_scales, offs):
    idx = unstriped(offs)
    xtu = unpack_weight(xt_words, xt_scales, "e2m1")
    wcu = unpack_weight(wc_words, wc_scales, "e4m3")
    wou = unpack_weight(wo_words, wo_scales, "e2m1")
    wsu = unpack_weight(ws_words, ws_scales, "e4m3")
    wcidxg = wcu[:, idx]
    z = xtu.T @ wcidxg
    p = np.exp(z)
    q = p / np.sum(p, axis=1, keepdims=True)
    qt = q.T
    qw = qt * f64(fj)
    qwq = mxq(qw, 0, "e4m3")
    y = wou.T @ qwq + wsu.T @ xtu
    words, scales = planes(y)
    return y, words, scales

@@ -1,0 +1,201 @@
+from contextlib import ExitStack
+
+import concourse.mybir as mybir
+from concourse.masks import make_identity
+
+K, T, C, J, N = 512, 512, 2048, 512, 512
+FLOPS = 2 * K * T * J + 2 * J * N * T + 2 * K * N * T
+
+F32 = mybir.dt.float32
+BF16 = mybir.dt.bfloat16
+I32 = mybir.dt.int32
+U32 = mybir.dt.uint32
+U16 = mybir.dt.uint16
+U8 = mybir.dt.uint8
+E4M3 = mybir.dt.float8_e4m3fn_x4
+E2M1 = mybir.dt.float4_e2m1fn_x4
+ALU = mybir.AluOpType
+ACT = mybir.ActivationFunctionType
+AXIS = mybir.AxisListType
+
+P = 128
+PACK = 4
+TILES = T // P
+
+
+def load_scale_rows(queues, plane, scales):
+    for quad in range(4):
+        queues[quad].dma_start(
+            out=plane[32 * quad : 32 * quad + 4, :].bitcast(I32),
+            in_=scales[0, 4 * quad : 4 * quad + 4, :].bitcast(I32),
+        )
+
+
+def tile_list_share_weighted_listed_rows_pl_kernel(
+    tc, xt_words, xt_scales, wc_words, wc_scales, fj, wo_words, wo_scales, ws_words, ws_scales, offs, out_0, out_1, out_2
+):
+    nc = tc.nc
+    with ExitStack() as ctx:
+        keep = ctx.enter_context(tc.tile_pool(name="keep", bufs=1))
+        work = ctx.enter_context(tc.tile_pool(name="work", bufs=2))
+        psum = ctx.enter_context(tc.psum_pool(name="psum", bufs=1))
+
+        offsets = keep.tile([P, J // 16], U16, name="offsets")
+        nc.sync.dma_start(offsets[:], offs)
+        wc_plane = keep.tile([P, C], U8, name="wc_plane", align_bytes=64)
+        nc.vector.memset(wc_plane[:].bitcast(I32), 0)
+        load_scale_rows([nc.scalar] * 4, wc_plane, wc_scales)
+        wc_table = keep.tile([P, C], I32, name="wc_table", align_bytes=64)
+        nc.sync.dma_start(out=wc_table[:], in_=wc_words[0].rearrange("p n t -> p (n t)").bitcast(I32))
+        xt_codes = keep.tile([P, 2 * T], U8, name="xt_codes", align_bytes=64)
+        nc.sync.dma_start(out=xt_codes[:].bitcast(I32), in_=xt_words[0].bitcast(I32))
+        xt_plane = keep.tile([P, T], U8, name="xt_plane", align_bytes=64)
+        nc.gpsimd.memset(xt_plane[:].bitcast(I32), 0)
+        load_scale_rows([nc.gpsimd, nc.sync, nc.sync, nc.scalar], xt_plane, xt_scales)
+        fj_rows = keep.tile([P, PACK], F32, name="fj_rows")
+        nc.gpsimd.dma_start(out=fj_rows[:], in_=fj.rearrange("(p r) o -> p (r o)", r=PACK))
+        identity = keep.tile([P, P], F32, name="identity", align_bytes=64)
+        make_identity(nc, identity[:])
+        w_planes = keep.tile([P, 2 * N], U8, name="w_planes", align_bytes=64)
+        nc.vector.memset(w_planes[:].bitcast(I32), 0)
+        wo_raw = keep.tile([P, 2 * N], U8, name="wo_raw", align_bytes=64)
+        nc.sync.dma_start(out=wo_raw[:].bitcast(I32), in_=wo_words[0].bitcast(I32))
+        ws_raw = keep.tile([P, N], I32, name="ws_raw", align_bytes=64)
+        nc.sync.dma_start(out=ws_raw[:], in_=ws_words[0].rearrange("p n t -> p (n t)").bitcast(I32))
+        load_scale_rows([nc.sync] * 4, w_planes[:, 0:N], ws_scales)
+        load_scale_rows([nc.gpsimd, nc.gpsimd, nc.sync, nc.sync], w_planes[:, N : 2 * N], wo_scales)
+
+        picked_plane = keep.tile([P, J], U8, name="picked_plane", align_bytes=64)
+        nc.vector.tensor_copy(out=picked_plane[:], in_=wc_plane[:].indirect(offsets[:]))
+        picked_codes = keep.tile([P, J], U32, name="picked_codes", align_bytes=64)
+        nc.vector.tensor_copy(out=picked_codes[:], in_=wc_table[:].bitcast(U32).indirect(offsets[:]))
+
+        y_codes = keep.tile([P, T], U32, name="y_codes", align_bytes=64)
+        y_plane = keep.tile([P, T], U8, name="y_plane", align_bytes=64)
+        y_banks = {}
+        shares = {}
+        turned = {}
+
+        def scores(i):
+            z = psum.tile([P, J], F32, name="z", tag="bank%d" % i)
+            nc.tensor.matmul_mx(
+                out=z[:],
+                lhsT=xt_codes[:, 2 * P * i : 2 * P * (i + 1)].bitcast(E2M1),
+                lhsT_scale=xt_plane[:, P * i : P * (i + 1)],
+                rhs=picked_codes[:].bitcast(E4M3),
+                rhs_scale=picked_plane[:],
+                start=True,
+                stop=True,
+            )
+            neg_top = work.tile([P, 1], F32, name="neg_top", bufs=4)
+            nc.vector.tensor_reduce(out=neg_top[:], in_=z[:], axis=AXIS.X, op=ALU.max, negate=True)
+            expz = work.tile([P, J], F32, name="expz", bufs=4)
+            total = work.tile([P, 1], F32, name="total", bufs=4)
+            nc.scalar.activation(
+                out=expz[:].rearrange("t (u p e) -> t u p e", u=2, e=2),
+                in_=z[:].rearrange("t (p u e) -> t u p e", u=2, e=2),
+                func=ACT.Exp,
+                bias=neg_top[:],
+                accum_out=total[:],
+            )
+            shares[i] = (expz, total)
+
+        def skip(i):
+            y_banks[i] = psum.tile([P, PACK, P], F32, name="y_bank", tag="bank%d" % ((i + 4) % 5))
+            for r in range(PACK):
+                nc.tensor.matmul_mx(
+                    out=y_banks[i][:, r, :],
+                    lhsT=ws_dealt[:, P * r : P * (r + 1)].bitcast(E4M3),
+                    lhsT_scale=planes_dealt[:, P * r : P * (r + 1)],
+                    rhs=xt_codes[:, 2 * P * i : 2 * P * (i + 1)].bitcast(E2M1),
+                    rhs_scale=xt_plane[:, P * i : P * (i + 1)],
+                    start=(r == 0),
+                    stop=False,
+                )
+
+        def weigh(i):
+            expz, total = shares[i]
+            inverse = work.tile([P, 1], F32, name="inverse", bufs=4)
+            nc.vector.reciprocal(out=inverse[:], in_=total[:])
+            qw = work.tile([P, J], BF16, name="qw", align_bytes=64, bufs=4)
+            nc.vector.scalar_tensor_tensor(
+                out=qw[:], in0=expz[:], scalar=inverse[:], in1=fj_spread, op0=ALU.mult, op1=ALU.mult
+            )
+            bank = psum.tile([P, 2, P], F32, name="turn_bank", tag="turn", bufs=2)
+            pairs = qw[:].bitcast(F32)
+            for u in range(2):
+                nc.tensor.transpose(bank[:, u, :], pairs[:, P * u : P * (u + 1)], identity[:])
+            grouped = work.tile([P, PACK * P], BF16, name="grouped", align_bytes=64, bufs=4)
+            nc.scalar.copy(
+                out=grouped[:].bitcast(F32).rearrange("p (t u) -> p t u", u=2),
+                in_=bank[:].rearrange("p u t -> p t u"),
+            )
+            turned[i] = grouped
+
+        def rows(i):
+            codes = work.tile([P, P], U32, name="codes", align_bytes=64, bufs=4)
+            plane = work.tile([P, P], U8, name="plane", align_bytes=64, bufs=4)
+            nc.vector.quantize_mx(out=codes[:].bitcast(E4M3), scales=plane[:], in_=turned[i][:])
+            for r in range(PACK):
+                nc.tensor.matmul_mx(
+                    out=y_banks[i][:, r, :],
+                    lhsT=wo_dealt[:, 2 * P * r : 2 * P * (r + 1)].bitcast(E2M1),
+                    lhsT_scale=planes_dealt[:, N + P * r : N + P * (r + 1)],
+                    rhs=codes[:].bitcast(E4M3),
+                    rhs_scale=plane[:],
+                    start=False,
+                    stop=(r == PACK - 1),
+                )
+
+        def hand_out(i):
+            cols = slice(P * i, P * (i + 1))
+            y = work.tile([P, PACK, P], F32, name="y", bufs=4)
+            nc.scalar.copy(out=y[:], in_=y_banks[i][:])
+            nc.sync.dma_start(out=out_0.rearrange("(p r) t -> p r t", r=PACK)[:, :, cols], in_=y[:])
+            rounded = work.tile([P, PACK * P], BF16, name="rounded", align_bytes=64, bufs=4)
+            nc.vector.tensor_copy(
+                out=rounded[:].rearrange("p (c i r) -> p c r i", i=4, r=PACK),
+                in_=y[:].rearrange("p r (c i) -> p c r i", i=4),
+            )
+            nc.vector.quantize_mx(out=y_codes[:, cols].bitcast(E4M3), scales=y_plane[:, cols], in_=rounded[:])
+            nc.sync.dma_start(
+                out=out_1[0].rearrange("p n t -> p (n t)").bitcast(I32)[:, cols], in_=y_codes[:, cols].bitcast(I32)
+            )
+
+        for i in range(TILES):
+            scores(i)
+        fj_bank = psum.tile([P, 2, P, 2], F32, name="fj_bank")
+        for r in range(PACK):
+            nc.tensor.transpose(fj_bank[:, r // 2, :, r % 2], fj_rows[:, r : r + 1].to_broadcast([P, P]), identity[:])
+        fj_spread = fj_bank[:].rearrange("t u p e -> t (u p e)")
+
+        for i in range(TILES):
+            weigh(i)
+        wo_dealt = keep.tile([P, 2 * N], U8, name="wo_dealt", align_bytes=64)
+        nc.gpsimd.tensor_copy(
+            out=wo_dealt[:].rearrange("p (r m b) -> p r m b", r=PACK, b=2),
+            in_=wo_raw[:].rearrange("p (m r b) -> p r m b", r=PACK, b=2),
+        )
+        ws_dealt = keep.tile([P, N], I32, name="ws_dealt", align_bytes=64)
+        nc.gpsimd.tensor_copy(
+            out=ws_dealt[:].rearrange("p (r c i) -> p c r i", r=PACK, i=4),
+            in_=ws_raw[:].rearrange("p (c i r) -> p c r i", r=PACK, i=4),
+        )
+        planes_dealt = keep.tile([P, 2 * N], U8, name="planes_dealt", align_bytes=64)
+        nc.gpsimd.tensor_copy(
+            out=planes_dealt[:].rearrange("p (w r m) -> p w r m", w=2, r=PACK),
+            in_=w_planes[:].rearrange("p (w m r) -> p w r m", w=2, r=PACK),
+        )
+
+        for i in range(TILES):
+            skip(i)
+        for i in range(TILES):
+            rows(i)
+        for i in range(TILES):
+            hand_out(i)
+        queues = [nc.scalar, nc.sync, nc.scalar, nc.sync]
+        for quad in range(4):
+            queues[quad].dma_start(
+                out=out_2[0, 4 * quad : 4 * quad + 4, :].bitcast(I32),
+                in_=y_plane[32 * quad : 32 * quad + 4, :].bitcast(I32),
+            )

@@ -42,33 +42,42 @@ def tile_list_share_weighted_listed_rows_pl_kernel(
 
         offsets = keep.tile([P, J // 16], U16, name="offsets")
         nc.sync.dma_start(offsets[:], offs)
+        fj_rows = keep.tile([P, PACK], F32, name="fj_rows")
+        nc.sync.dma_start(out=fj_rows[:], in_=fj.rearrange("(p r) o -> p (r o)", r=PACK))
         wc_plane = keep.tile([P, C], U8, name="wc_plane", align_bytes=64)
         nc.vector.memset(wc_plane[:].bitcast(I32), 0)
-        load_scale_rows([nc.scalar] * 4, wc_plane, wc_scales)
+        load_scale_rows([nc.sync, nc.sync, nc.scalar, nc.scalar], wc_plane, wc_scales)
         wc_table = keep.tile([P, C], I32, name="wc_table", align_bytes=64)
         nc.sync.dma_start(out=wc_table[:], in_=wc_words[0].rearrange("p n t -> p (n t)").bitcast(I32))
         xt_codes = keep.tile([P, 2 * T], U8, name="xt_codes", align_bytes=64)
         nc.sync.dma_start(out=xt_codes[:].bitcast(I32), in_=xt_words[0].bitcast(I32))
         xt_plane = keep.tile([P, T], U8, name="xt_plane", align_bytes=64)
-        nc.gpsimd.memset(xt_plane[:].bitcast(I32), 0)
-        load_scale_rows([nc.gpsimd, nc.sync, nc.sync, nc.scalar], xt_plane, xt_scales)
-        fj_rows = keep.tile([P, PACK], F32, name="fj_rows")
-        nc.gpsimd.dma_start(out=fj_rows[:], in_=fj.rearrange("(p r) o -> p (r o)", r=PACK))
+        nc.vector.memset(xt_plane[:].bitcast(I32), 0)
+        load_scale_rows([nc.sync] * 4, xt_plane, xt_scales)
         identity = keep.tile([P, P], F32, name="identity", align_bytes=64)
         make_identity(nc, identity[:])
         w_planes = keep.tile([P, 2 * N], U8, name="w_planes", align_bytes=64)
         nc.vector.memset(w_planes[:].bitcast(I32), 0)
-        wo_raw = keep.tile([P, 2 * N], U8, name="wo_raw", align_bytes=64)
-        nc.sync.dma_start(out=wo_raw[:].bitcast(I32), in_=wo_words[0].bitcast(I32))
         ws_raw = keep.tile([P, N], I32, name="ws_raw", align_bytes=64)
         nc.sync.dma_start(out=ws_raw[:], in_=ws_words[0].rearrange("p n t -> p (n t)").bitcast(I32))
+        wo_raw = keep.tile([P, 2 * N], U8, name="wo_raw", align_bytes=64)
+        nc.sync.dma_start(out=wo_raw[:].bitcast(I32), in_=wo_words[0].bitcast(I32))
         load_scale_rows([nc.sync] * 4, w_planes[:, 0:N], ws_scales)
-        load_scale_rows([nc.gpsimd, nc.gpsimd, nc.sync, nc.sync], w_planes[:, N : 2 * N], wo_scales)
+        load_scale_rows([nc.sync] * 4, w_planes[:, N : 2 * N], wo_scales)
 
         picked_plane = keep.tile([P, J], U8, name="picked_plane", align_bytes=64)
         nc.vector.tensor_copy(out=picked_plane[:], in_=wc_plane[:].indirect(offsets[:]))
         picked_codes = keep.tile([P, J], U32, name="picked_codes", align_bytes=64)
-        nc.vector.tensor_copy(out=picked_codes[:], in_=wc_table[:].bitcast(U32).indirect(offsets[:]))
+        for half in range(2):
+            nc.vector.tensor_copy(
+                out=picked_codes[:, 256 * half : 256 * (half + 1)],
+                in_=wc_table[:].bitcast(U32).indirect(offsets[:, 16 * half : 16 * (half + 1)]),
+            )
+
+        fj_bank = psum.tile([P, 2, P, 2], F32, name="fj_bank")
+        for r in range(PACK):
+            nc.tensor.transpose(fj_bank[:, r // 2, :, r % 2], fj_rows[:, r : r + 1].to_broadcast([P, P]), identity[:])
+        fj_spread = fj_bank[:].rearrange("t u p e -> t (u p e)")
 
         y_codes = keep.tile([P, T], U32, name="y_codes", align_bytes=64)
         y_plane = keep.tile([P, T], U8, name="y_plane", align_bytes=64)
@@ -78,15 +87,17 @@ def tile_list_share_weighted_listed_rows_pl_kernel(
 
         def scores(i):
             z = psum.tile([P, J], F32, name="z", tag="bank%d" % i)
-            nc.tensor.matmul_mx(
-                out=z[:],
-                lhsT=xt_codes[:, 2 * P * i : 2 * P * (i + 1)].bitcast(E2M1),
-                lhsT_scale=xt_plane[:, P * i : P * (i + 1)],
-                rhs=picked_codes[:].bitcast(E4M3),
-                rhs_scale=picked_plane[:],
-                start=True,
-                stop=True,
-            )
+            width = J // 2 if i == 0 else J
+            for j0 in range(0, J, width):
+                nc.tensor.matmul_mx(
+                    out=z[:, j0 : j0 + width],
+                    lhsT=xt_codes[:, 2 * P * i : 2 * P * (i + 1)].bitcast(E2M1),
+                    lhsT_scale=xt_plane[:, P * i : P * (i + 1)],
+                    rhs=picked_codes[:, j0 : j0 + width].bitcast(E4M3),
+                    rhs_scale=picked_plane[:, j0 : j0 + width],
+                    start=True,
+                    stop=True,
+                )
             neg_top = work.tile([P, 1], F32, name="neg_top", bufs=4)
             nc.vector.tensor_reduce(out=neg_top[:], in_=z[:], axis=AXIS.X, op=ALU.max, negate=True)
             expz = work.tile([P, J], F32, name="expz", bufs=4)
@@ -98,25 +109,32 @@ def tile_list_share_weighted_listed_rows_pl_kernel(
                 bias=neg_top[:],
                 accum_out=total[:],
             )
-            shares[i] = (expz, total)
-
-        def skip(i):
-            y_banks[i] = psum.tile([P, PACK, P], F32, name="y_bank", tag="bank%d" % ((i + 4) % 5))
-            for r in range(PACK):
-                nc.tensor.matmul_mx(
-                    out=y_banks[i][:, r, :],
-                    lhsT=ws_dealt[:, P * r : P * (r + 1)].bitcast(E4M3),
-                    lhsT_scale=planes_dealt[:, P * r : P * (r + 1)],
-                    rhs=xt_codes[:, 2 * P * i : 2 * P * (i + 1)].bitcast(E2M1),
-                    rhs_scale=xt_plane[:, P * i : P * (i + 1)],
-                    start=(r == 0),
-                    stop=False,
-                )
-
-        def weigh(i):
-            expz, total = shares[i]
             inverse = work.tile([P, 1], F32, name="inverse", bufs=4)
             nc.vector.reciprocal(out=inverse[:], in_=total[:])
+            shares[i] = (expz, inverse)
+
+        def skip(i):
+            if i < TILES - 1:
+                whole = psum.tile([P, PACK, P], F32, name="y_bank", tag="bank%d" % ((i + 4) % 5))
+                y_banks[i] = [(whole, range(PACK))]
+            else:
+                low = psum.tile([P, 2, P], F32, name="y_low", tag="bank2")
+                high = psum.tile([P, 2, P], F32, name="y_high", tag="bank3")
+                y_banks[i] = [(low, range(0, 2)), (high, range(2, 4))]
+            for bank, slices in y_banks[i]:
+                for r in slices:
+                    nc.tensor.matmul_mx(
+                        out=bank[:, r - slices[0], :],
+                        lhsT=ws_dealt[:, P * r : P * (r + 1)].bitcast(E4M3),
+                        lhsT_scale=planes_dealt[:, P * r : P * (r + 1)],
+                        rhs=xt_codes[:, 2 * P * i : 2 * P * (i + 1)].bitcast(E2M1),
+                        rhs_scale=xt_plane[:, P * i : P * (i + 1)],
+                        start=(r == slices[0]),
+                        stop=False,
+                    )
+
+        def weigh(i):
+            expz, inverse = shares[i]
             qw = work.tile([P, J], BF16, name="qw", align_bytes=64, bufs=4)
             nc.vector.scalar_tensor_tensor(
                 out=qw[:], in0=expz[:], scalar=inverse[:], in1=fj_spread, op0=ALU.mult, op1=ALU.mult
@@ -136,64 +154,82 @@ def tile_list_share_weighted_listed_rows_pl_kernel(
             codes = work.tile([P, P], U32, name="codes", align_bytes=64, bufs=4)
             plane = work.tile([P, P], U8, name="plane", align_bytes=64, bufs=4)
             nc.vector.quantize_mx(out=codes[:].bitcast(E4M3), scales=plane[:], in_=turned[i][:])
-            for r in range(PACK):
-                nc.tensor.matmul_mx(
-                    out=y_banks[i][:, r, :],
-                    lhsT=wo_dealt[:, 2 * P * r : 2 * P * (r + 1)].bitcast(E2M1),
-                    lhsT_scale=planes_dealt[:, N + P * r : N + P * (r + 1)],
-                    rhs=codes[:].bitcast(E4M3),
-                    rhs_scale=plane[:],
-                    start=False,
-                    stop=(r == PACK - 1),
-                )
+            for bank, slices in y_banks[i]:
+                for r in slices:
+                    nc.tensor.matmul_mx(
+                        out=bank[:, r - slices[0], :],
+                        lhsT=wo_dealt[:, 2 * P * r : 2 * P * (r + 1)].bitcast(E2M1),
+                        lhsT_scale=planes_dealt[:, N + P * r : N + P * (r + 1)],
+                        rhs=codes[:].bitcast(E4M3),
+                        rhs_scale=plane[:],
+                        start=False,
+                        stop=(r == slices[-1]),
+                    )
+
+        rounded = keep.tile([P, PACK * T], BF16, name="rounded", align_bytes=64)
 
         def hand_out(i):
             cols = slice(P * i, P * (i + 1))
             y = work.tile([P, PACK, P], F32, name="y", bufs=4)
-            nc.scalar.copy(out=y[:], in_=y_banks[i][:])
+            for (bank, slices), copy in zip(y_banks[i], (nc.scalar.copy, nc.vector.tensor_copy)):
+                copy(out=y[:, slices[0] : slices[-1] + 1, :], in_=bank[:])
             nc.sync.dma_start(out=out_0.rearrange("(p r) t -> p r t", r=PACK)[:, :, cols], in_=y[:])
-            rounded = work.tile([P, PACK * P], BF16, name="rounded", align_bytes=64, bufs=4)
             nc.vector.tensor_copy(
-                out=rounded[:].rearrange("p (c i r) -> p c r i", i=4, r=PACK),
+                out=rounded[:, PACK * P * i : PACK * P * (i + 1)].rearrange("p (c i r) -> p c r i", i=4, r=PACK),
                 in_=y[:].rearrange("p r (c i) -> p c r i", i=4),
             )
-            nc.vector.quantize_mx(out=y_codes[:, cols].bitcast(E4M3), scales=y_plane[:, cols], in_=rounded[:])
+
+        def quantise_y(first, last):
+            cols = slice(P * first, P * last)
+            nc.vector.quantize_mx(
+                out=y_codes[:, cols].bitcast(E4M3),
+                scales=y_plane[:, cols],
+                in_=rounded[:, PACK * P * first : PACK * P * last],
+            )
+
+        def store_codes(first, last):
+            cols = slice(P * first, P * last)
             nc.sync.dma_start(
                 out=out_1[0].rearrange("p n t -> p (n t)").bitcast(I32)[:, cols], in_=y_codes[:, cols].bitcast(I32)
             )
 
         for i in range(TILES):
             scores(i)
-        fj_bank = psum.tile([P, 2, P, 2], F32, name="fj_bank")
-        for r in range(PACK):
-            nc.tensor.transpose(fj_bank[:, r // 2, :, r % 2], fj_rows[:, r : r + 1].to_broadcast([P, P]), identity[:])
-        fj_spread = fj_bank[:].rearrange("t u p e -> t (u p e)")
-
-        for i in range(TILES):
+        for i in range(TILES - 1):
             weigh(i)
-        wo_dealt = keep.tile([P, 2 * N], U8, name="wo_dealt", align_bytes=64)
-        nc.gpsimd.tensor_copy(
-            out=wo_dealt[:].rearrange("p (r m b) -> p r m b", r=PACK, b=2),
-            in_=wo_raw[:].rearrange("p (m r b) -> p r m b", r=PACK, b=2),
-        )
-        ws_dealt = keep.tile([P, N], I32, name="ws_dealt", align_bytes=64)
-        nc.gpsimd.tensor_copy(
+        ws_dealt = keep.tile([P, N], U32, name="ws_dealt", align_bytes=64)
+        nc.scalar.copy(
             out=ws_dealt[:].rearrange("p (r c i) -> p c r i", r=PACK, i=4),
-            in_=ws_raw[:].rearrange("p (c i r) -> p c r i", r=PACK, i=4),
+            in_=ws_raw[:].bitcast(U32).rearrange("p (c i r) -> p c r i", r=PACK, i=4),
+        )
+        wo_dealt = keep.tile([P, 2 * N], U8, name="wo_dealt", align_bytes=64)
+        nc.scalar.copy(
+            out=wo_dealt[:].bitcast(U16).rearrange("p (r m) -> p r m", r=PACK),
+            in_=wo_raw[:].bitcast(U16).rearrange("p (m r) -> p r m", r=PACK),
         )
         planes_dealt = keep.tile([P, 2 * N], U8, name="planes_dealt", align_bytes=64)
-        nc.gpsimd.tensor_copy(
-            out=planes_dealt[:].rearrange("p (w r m) -> p w r m", w=2, r=PACK),
-            in_=w_planes[:].rearrange("p (w m r) -> p w r m", w=2, r=PACK),
-        )
+        for w in range(2):
+            nc.gpsimd.tensor_copy(
+                out=planes_dealt[:, N * w : N * (w + 1)].rearrange("p (r c i) -> p c r i", r=PACK, i=16),
+                in_=w_planes[:, N * w : N * (w + 1)].rearrange("p (c i r) -> p c r i", r=PACK, i=16),
+            )
 
         for i in range(TILES):
             skip(i)
-        for i in range(TILES):
+        rows(0)
+        weigh(3)
+        for i in range(1, TILES):
             rows(i)
-        for i in range(TILES):
-            hand_out(i)
-        queues = [nc.scalar, nc.sync, nc.scalar, nc.sync]
+        hand_out(0)
+        hand_out(1)
+        quantise_y(0, 2)
+        store_codes(0, 2)
+        hand_out(2)
+        quantise_y(2, 3)
+        hand_out(3)
+        quantise_y(3, 4)
+        store_codes(2, 4)
+        queues = [nc.scalar, nc.scalar, nc.sync, nc.scalar]
         for quad in range(4):
             queues[quad].dma_start(
                 out=out_2[0, 4 * quad : 4 * quad + 4, :].bitcast(I32),

@@ -79,6 +79,8 @@ def tile_list_share_weighted_listed_rows_pl_kernel(
             nc.tensor.transpose(fj_bank[:, r // 2, :, r % 2], fj_rows[:, r : r + 1].to_broadcast([P, P]), identity[:])
         fj_spread = fj_bank[:].rearrange("t u p e -> t (u p e)")
 
+        minus_one = keep.tile([P, 1], F32, name="minus_one")
+        nc.gpsimd.memset(minus_one[:], -1.0)
         y_codes = keep.tile([P, T], U32, name="y_codes", align_bytes=64)
         y_plane = keep.tile([P, T], U8, name="y_plane", align_bytes=64)
         y_banks = {}
@@ -110,7 +112,10 @@ def tile_list_share_weighted_listed_rows_pl_kernel(
                 accum_out=total[:],
             )
             inverse = work.tile([P, 1], F32, name="inverse", bufs=4)
-            nc.vector.reciprocal(out=inverse[:], in_=total[:])
+            if i < 2:
+                nc.vector.reciprocal(out=inverse[:], in_=total[:])
+            else:
+                nc.gpsimd.tensor_tensor(out=inverse[:], in0=total[:], in1=minus_one[:], op=ALU.pow)
             shares[i] = (expz, inverse)
 
         def skip(i):
@@ -220,15 +225,11 @@ def tile_list_share_weighted_listed_rows_pl_kernel(
         weigh(3)
         for i in range(1, TILES):
             rows(i)
-        hand_out(0)
-        hand_out(1)
-        quantise_y(0, 2)
-        store_codes(0, 2)
-        hand_out(2)
-        quantise_y(2, 3)
-        hand_out(3)
-        quantise_y(3, 4)
-        store_codes(2, 4)
+        for i in range(TILES):
+            hand_out(i)
+        for first in (0, 2):
+            quantise_y(first, first + 2)
+            store_codes(first, first + 2)
         queues = [nc.scalar, nc.scalar, nc.sync, nc.scalar]
         for quad in range(4):
             queues[quad].dma_start(

@@ -20,15 +20,22 @@ AXIS = mybir.AxisListType
 
 P = 128
 PACK = 4
+QUADS = 4
+GROUP = 16
 TILES = T // P
+LAST = TILES - 1
+HALF = J // 2
+VECTOR_INVERSES = 2
+
+
+def quad_rows(quad):
+    return slice(32 * quad, 32 * quad + 4), slice(4 * quad, 4 * quad + 4)
 
 
 def load_scale_rows(queues, plane, scales):
-    for quad in range(4):
-        queues[quad].dma_start(
-            out=plane[32 * quad : 32 * quad + 4, :].bitcast(I32),
-            in_=scales[0, 4 * quad : 4 * quad + 4, :].bitcast(I32),
-        )
+    for quad in range(QUADS):
+        partitions, scale_rows = quad_rows(quad)
+        queues[quad].dma_start(out=plane[partitions, :].bitcast(I32), in_=scales[0, scale_rows, :].bitcast(I32))
 
 
 def tile_list_share_weighted_listed_rows_pl_kernel(
@@ -37,10 +44,10 @@ def tile_list_share_weighted_listed_rows_pl_kernel(
     nc = tc.nc
     with ExitStack() as ctx:
         keep = ctx.enter_context(tc.tile_pool(name="keep", bufs=1))
-        work = ctx.enter_context(tc.tile_pool(name="work", bufs=2))
+        work = ctx.enter_context(tc.tile_pool(name="work", bufs=TILES))
         psum = ctx.enter_context(tc.psum_pool(name="psum", bufs=1))
 
-        offsets = keep.tile([P, J // 16], U16, name="offsets")
+        offsets = keep.tile([P, J // GROUP], U16, name="offsets")
         nc.sync.dma_start(offsets[:], offs)
         fj_rows = keep.tile([P, PACK], F32, name="fj_rows")
         nc.sync.dma_start(out=fj_rows[:], in_=fj.rearrange("(p r) o -> p (r o)", r=PACK))
@@ -53,7 +60,7 @@ def tile_list_share_weighted_listed_rows_pl_kernel(
         nc.sync.dma_start(out=xt_codes[:].bitcast(I32), in_=xt_words[0].bitcast(I32))
         xt_plane = keep.tile([P, T], U8, name="xt_plane", align_bytes=64)
         nc.vector.memset(xt_plane[:].bitcast(I32), 0)
-        load_scale_rows([nc.sync] * 4, xt_plane, xt_scales)
+        load_scale_rows([nc.sync] * QUADS, xt_plane, xt_scales)
         identity = keep.tile([P, P], F32, name="identity", align_bytes=64)
         make_identity(nc, identity[:])
         w_planes = keep.tile([P, 2 * N], U8, name="w_planes", align_bytes=64)
@@ -62,16 +69,16 @@ def tile_list_share_weighted_listed_rows_pl_kernel(
         nc.sync.dma_start(out=ws_raw[:], in_=ws_words[0].rearrange("p n t -> p (n t)").bitcast(I32))
         wo_raw = keep.tile([P, 2 * N], U8, name="wo_raw", align_bytes=64)
         nc.sync.dma_start(out=wo_raw[:].bitcast(I32), in_=wo_words[0].bitcast(I32))
-        load_scale_rows([nc.sync] * 4, w_planes[:, 0:N], ws_scales)
-        load_scale_rows([nc.sync] * 4, w_planes[:, N : 2 * N], wo_scales)
+        load_scale_rows([nc.sync] * QUADS, w_planes[:, 0:N], ws_scales)
+        load_scale_rows([nc.sync] * QUADS, w_planes[:, N : 2 * N], wo_scales)
 
         picked_plane = keep.tile([P, J], U8, name="picked_plane", align_bytes=64)
         nc.vector.tensor_copy(out=picked_plane[:], in_=wc_plane[:].indirect(offsets[:]))
         picked_codes = keep.tile([P, J], U32, name="picked_codes", align_bytes=64)
-        for half in range(2):
+        for j0 in range(0, J, HALF):
             nc.vector.tensor_copy(
-                out=picked_codes[:, 256 * half : 256 * (half + 1)],
-                in_=wc_table[:].bitcast(U32).indirect(offsets[:, 16 * half : 16 * (half + 1)]),
+                out=picked_codes[:, j0 : j0 + HALF],
+                in_=wc_table[:].bitcast(U32).indirect(offsets[:, j0 // GROUP : (j0 + HALF) // GROUP]),
             )
 
         fj_bank = psum.tile([P, 2, P, 2], F32, name="fj_bank")
@@ -87,9 +94,10 @@ def tile_list_share_weighted_listed_rows_pl_kernel(
         shares = {}
         turned = {}
 
+
         def scores(i):
             z = psum.tile([P, J], F32, name="z", tag="bank%d" % i)
-            width = J // 2 if i == 0 else J
+            width = HALF if i == 0 else J
             for j0 in range(0, J, width):
                 nc.tensor.matmul_mx(
                     out=z[:, j0 : j0 + width],
@@ -100,10 +108,10 @@ def tile_list_share_weighted_listed_rows_pl_kernel(
                     start=True,
                     stop=True,
                 )
-            neg_top = work.tile([P, 1], F32, name="neg_top", bufs=4)
+            neg_top = work.tile([P, 1], F32, name="neg_top")
             nc.vector.tensor_reduce(out=neg_top[:], in_=z[:], axis=AXIS.X, op=ALU.max, negate=True)
-            expz = work.tile([P, J], F32, name="expz", bufs=4)
-            total = work.tile([P, 1], F32, name="total", bufs=4)
+            expz = work.tile([P, J], F32, name="expz")
+            total = work.tile([P, 1], F32, name="total")
             nc.scalar.activation(
                 out=expz[:].rearrange("t (u p e) -> t u p e", u=2, e=2),
                 in_=z[:].rearrange("t (p u e) -> t u p e", u=2, e=2),
@@ -111,21 +119,21 @@ def tile_list_share_weighted_listed_rows_pl_kernel(
                 bias=neg_top[:],
                 accum_out=total[:],
             )
-            inverse = work.tile([P, 1], F32, name="inverse", bufs=4)
-            if i < 2:
+            inverse = work.tile([P, 1], F32, name="inverse")
+            if i < VECTOR_INVERSES:
                 nc.vector.reciprocal(out=inverse[:], in_=total[:])
             else:
                 nc.gpsimd.tensor_tensor(out=inverse[:], in0=total[:], in1=minus_one[:], op=ALU.pow)
             shares[i] = (expz, inverse)
 
         def skip(i):
-            if i < TILES - 1:
-                whole = psum.tile([P, PACK, P], F32, name="y_bank", tag="bank%d" % ((i + 4) % 5))
+            if i < LAST:
+                whole = psum.tile([P, PACK, P], F32, name="y_bank", tag="bank%d" % ((i + TILES) % (TILES + 1)))
                 y_banks[i] = [(whole, range(PACK))]
             else:
                 low = psum.tile([P, 2, P], F32, name="y_low", tag="bank2")
                 high = psum.tile([P, 2, P], F32, name="y_high", tag="bank3")
-                y_banks[i] = [(low, range(0, 2)), (high, range(2, 4))]
+                y_banks[i] = [(low, range(0, 2)), (high, range(2, PACK))]
             for bank, slices in y_banks[i]:
                 for r in slices:
                     nc.tensor.matmul_mx(
@@ -140,7 +148,7 @@ def tile_list_share_weighted_listed_rows_pl_kernel(
 
         def weigh(i):
             expz, inverse = shares[i]
-            qw = work.tile([P, J], BF16, name="qw", align_bytes=64, bufs=4)
+            qw = work.tile([P, J], BF16, name="qw", align_bytes=64)
             nc.vector.scalar_tensor_tensor(
                 out=qw[:], in0=expz[:], scalar=inverse[:], in1=fj_spread, op0=ALU.mult, op1=ALU.mult
             )
@@ -148,7 +156,7 @@ def tile_list_share_weighted_listed_rows_pl_kernel(
             pairs = qw[:].bitcast(F32)
             for u in range(2):
                 nc.tensor.transpose(bank[:, u, :], pairs[:, P * u : P * (u + 1)], identity[:])
-            grouped = work.tile([P, PACK * P], BF16, name="grouped", align_bytes=64, bufs=4)
+            grouped = work.tile([P, PACK * P], BF16, name="grouped", align_bytes=64)
             nc.scalar.copy(
                 out=grouped[:].bitcast(F32).rearrange("p (t u) -> p t u", u=2),
                 in_=bank[:].rearrange("p u t -> p t u"),
@@ -156,8 +164,8 @@ def tile_list_share_weighted_listed_rows_pl_kernel(
             turned[i] = grouped
 
         def rows(i):
-            codes = work.tile([P, P], U32, name="codes", align_bytes=64, bufs=4)
-            plane = work.tile([P, P], U8, name="plane", align_bytes=64, bufs=4)
+            codes = work.tile([P, P], U32, name="codes", align_bytes=64)
+            plane = work.tile([P, P], U8, name="plane", align_bytes=64)
             nc.vector.quantize_mx(out=codes[:].bitcast(E4M3), scales=plane[:], in_=turned[i][:])
             for bank, slices in y_banks[i]:
                 for r in slices:
@@ -175,37 +183,35 @@ def tile_list_share_weighted_listed_rows_pl_kernel(
 
         def hand_out(i):
             cols = slice(P * i, P * (i + 1))
-            y = work.tile([P, PACK, P], F32, name="y", bufs=4)
-            for (bank, slices), copy in zip(y_banks[i], (nc.scalar.copy, nc.vector.tensor_copy)):
-                copy(out=y[:, slices[0] : slices[-1] + 1, :], in_=bank[:])
+            y = work.tile([P, PACK, P], F32, name="y")
+            for bank, slices in y_banks[i]:
+                nc.scalar.copy(out=y[:, slices[0] : slices[-1] + 1, :], in_=bank[:])
             nc.sync.dma_start(out=out_0.rearrange("(p r) t -> p r t", r=PACK)[:, :, cols], in_=y[:])
             nc.vector.tensor_copy(
-                out=rounded[:, PACK * P * i : PACK * P * (i + 1)].rearrange("p (c i r) -> p c r i", i=4, r=PACK),
-                in_=y[:].rearrange("p r (c i) -> p c r i", i=4),
+                out=rounded[:, PACK * P * i : PACK * P * (i + 1)].rearrange("p (c a r) -> p c r a", a=4, r=PACK),
+                in_=y[:].rearrange("p r (c a) -> p c r a", a=4),
             )
 
-        def quantise_y(first, last):
+        def hand_out_codes(first, last):
             cols = slice(P * first, P * last)
             nc.vector.quantize_mx(
                 out=y_codes[:, cols].bitcast(E4M3),
                 scales=y_plane[:, cols],
                 in_=rounded[:, PACK * P * first : PACK * P * last],
             )
-
-        def store_codes(first, last):
-            cols = slice(P * first, P * last)
             nc.sync.dma_start(
                 out=out_1[0].rearrange("p n t -> p (n t)").bitcast(I32)[:, cols], in_=y_codes[:, cols].bitcast(I32)
             )
 
         for i in range(TILES):
             scores(i)
-        for i in range(TILES - 1):
+        for i in range(LAST):
             weigh(i)
+
         ws_dealt = keep.tile([P, N], U32, name="ws_dealt", align_bytes=64)
         nc.scalar.copy(
-            out=ws_dealt[:].rearrange("p (r c i) -> p c r i", r=PACK, i=4),
-            in_=ws_raw[:].bitcast(U32).rearrange("p (c i r) -> p c r i", r=PACK, i=4),
+            out=ws_dealt[:].rearrange("p (r c a) -> p c r a", r=PACK, a=4),
+            in_=ws_raw[:].bitcast(U32).rearrange("p (c a r) -> p c r a", r=PACK, a=4),
         )
         wo_dealt = keep.tile([P, 2 * N], U8, name="wo_dealt", align_bytes=64)
         nc.scalar.copy(
@@ -213,26 +219,23 @@ def tile_list_share_weighted_listed_rows_pl_kernel(
             in_=wo_raw[:].bitcast(U16).rearrange("p (m r) -> p r m", r=PACK),
         )
         planes_dealt = keep.tile([P, 2 * N], U8, name="planes_dealt", align_bytes=64)
-        for w in range(2):
+        for n0 in (0, N):
             nc.gpsimd.tensor_copy(
-                out=planes_dealt[:, N * w : N * (w + 1)].rearrange("p (r c i) -> p c r i", r=PACK, i=16),
-                in_=w_planes[:, N * w : N * (w + 1)].rearrange("p (c i r) -> p c r i", r=PACK, i=16),
+                out=planes_dealt[:, n0 : n0 + N].rearrange("p (r c a) -> p c r a", r=PACK, a=16),
+                in_=w_planes[:, n0 : n0 + N].rearrange("p (c a r) -> p c r a", r=PACK, a=16),
             )
 
         for i in range(TILES):
             skip(i)
         rows(0)
-        weigh(3)
+        weigh(LAST)
         for i in range(1, TILES):
             rows(i)
         for i in range(TILES):
             hand_out(i)
-        for first in (0, 2):
-            quantise_y(first, first + 2)
-            store_codes(first, first + 2)
+        for first in range(0, TILES, 2):
+            hand_out_codes(first, first + 2)
         queues = [nc.scalar, nc.scalar, nc.sync, nc.scalar]
-        for quad in range(4):
-            queues[quad].dma_start(
-                out=out_2[0, 4 * quad : 4 * quad + 4, :].bitcast(I32),
-                in_=y_plane[32 * quad : 32 * quad + 4, :].bitcast(I32),
-            )
+        for quad in range(QUADS):
+            partitions, scale_rows = quad_rows(quad)
+            queues[quad].dma_start(out=out_2[0, scale_rows, :].bitcast(I32), in_=y_plane[partitions, :].bitcast(I32))

from contextlib import ExitStack

import concourse.mybir as mybir
from concourse.masks import make_identity

K, T, C, J, N = 512, 512, 2048, 512, 512
FLOPS = 2 * K * T * J + 2 * J * N * T + 2 * K * N * T

F32 = mybir.dt.float32
BF16 = mybir.dt.bfloat16
I32 = mybir.dt.int32
U32 = mybir.dt.uint32
U16 = mybir.dt.uint16
U8 = mybir.dt.uint8
E4M3 = mybir.dt.float8_e4m3fn_x4
E2M1 = mybir.dt.float4_e2m1fn_x4
ALU = mybir.AluOpType
ACT = mybir.ActivationFunctionType
AXIS = mybir.AxisListType

P = 128
PACK = 4
QUADS = 4
GROUP = 16
TILES = T // P
LAST = TILES - 1
HALF = J // 2
VECTOR_INVERSES = 2


def quad_rows(quad):
    return slice(32 * quad, 32 * quad + 4), slice(4 * quad, 4 * quad + 4)


def load_scale_rows(queues, plane, scales):
    for quad in range(QUADS):
        partitions, scale_rows = quad_rows(quad)
        queues[quad].dma_start(out=plane[partitions, :].bitcast(I32), in_=scales[0, scale_rows, :].bitcast(I32))


def tile_list_share_weighted_listed_rows_pl_kernel(
    tc, xt_words, xt_scales, wc_words, wc_scales, fj, wo_words, wo_scales, ws_words, ws_scales, offs, out_0, out_1, out_2
):
    nc = tc.nc
    with ExitStack() as ctx:
        keep = ctx.enter_context(tc.tile_pool(name="keep", bufs=1))
        work = ctx.enter_context(tc.tile_pool(name="work", bufs=TILES))
        psum = ctx.enter_context(tc.psum_pool(name="psum", bufs=1))

        offsets = keep.tile([P, J // GROUP], U16, name="offsets")
        nc.sync.dma_start(offsets[:], offs)
        fj_rows = keep.tile([P, PACK], F32, name="fj_rows")
        nc.sync.dma_start(out=fj_rows[:], in_=fj.rearrange("(p r) o -> p (r o)", r=PACK))
        wc_plane = keep.tile([P, C], U8, name="wc_plane", align_bytes=64)
        nc.vector.memset(wc_plane[:].bitcast(I32), 0)
        load_scale_rows([nc.sync, nc.sync, nc.scalar, nc.scalar], wc_plane, wc_scales)
        wc_table = keep.tile([P, C], I32, name="wc_table", align_bytes=64)
        nc.sync.dma_start(out=wc_table[:], in_=wc_words[0].rearrange("p n t -> p (n t)").bitcast(I32))
        xt_codes = keep.tile([P, 2 * T], U8, name="xt_codes", align_bytes=64)
        nc.sync.dma_start(out=xt_codes[:].bitcast(I32), in_=xt_words[0].bitcast(I32))
        xt_plane = keep.tile([P, T], U8, name="xt_plane", align_bytes=64)
        nc.vector.memset(xt_plane[:].bitcast(I32), 0)
        load_scale_rows([nc.sync] * QUADS, xt_plane, xt_scales)
        identity = keep.tile([P, P], F32, name="identity", align_bytes=64)
        make_identity(nc, identity[:])
        w_planes = keep.tile([P, 2 * N], U8, name="w_planes", align_bytes=64)
        nc.vector.memset(w_planes[:].bitcast(I32), 0)
        ws_raw = keep.tile([P, N], I32, name="ws_raw", align_bytes=64)
        nc.sync.dma_start(out=ws_raw[:], in_=ws_words[0].rearrange("p n t -> p (n t)").bitcast(I32))
        wo_raw = keep.tile([P, 2 * N], U8, name="wo_raw", align_bytes=64)
        nc.sync.dma_start(out=wo_raw[:].bitcast(I32), in_=wo_words[0].bitcast(I32))
        load_scale_rows([nc.sync] * QUADS, w_planes[:, 0:N], ws_scales)
        load_scale_rows([nc.sync] * QUADS, w_planes[:, N : 2 * N], wo_scales)

        picked_plane = keep.tile([P, J], U8, name="picked_plane", align_bytes=64)
        nc.vector.tensor_copy(out=picked_plane[:], in_=wc_plane[:].indirect(offsets[:]))
        picked_codes = keep.tile([P, J], U32, name="picked_codes", align_bytes=64)
        for j0 in range(0, J, HALF):
            nc.vector.tensor_copy(
                out=picked_codes[:, j0 : j0 + HALF],
                in_=wc_table[:].bitcast(U32).indirect(offsets[:, j0 // GROUP : (j0 + HALF) // GROUP]),
            )

        fj_bank = psum.tile([P, 2, P, 2], F32, name="fj_bank")
        for r in range(PACK):
            nc.tensor.transpose(fj_bank[:, r // 2, :, r % 2], fj_rows[:, r : r + 1].to_broadcast([P, P]), identity[:])
        fj_spread = fj_bank[:].rearrange("t u p e -> t (u p e)")

        minus_one = keep.tile([P, 1], F32, name="minus_one")
        nc.gpsimd.memset(minus_one[:], -1.0)
        y_codes = keep.tile([P, T], U32, name="y_codes", align_bytes=64)
        y_plane = keep.tile([P, T], U8, name="y_plane", align_bytes=64)
        y_banks = {}
        shares = {}
        turned = {}


        def scores(i):
            z = psum.tile([P, J], F32, name="z", tag="bank%d" % i)
            width = HALF if i == 0 else J
            for j0 in range(0, J, width):
                nc.tensor.matmul_mx(
                    out=z[:, j0 : j0 + width],
                    lhsT=xt_codes[:, 2 * P * i : 2 * P * (i + 1)].bitcast(E2M1),
                    lhsT_scale=xt_plane[:, P * i : P * (i + 1)],
                    rhs=picked_codes[:, j0 : j0 + width].bitcast(E4M3),
                    rhs_scale=picked_plane[:, j0 : j0 + width],
                    start=True,
                    stop=True,
                )
            neg_top = work.tile([P, 1], F32, name="neg_top")
            nc.vector.tensor_reduce(out=neg_top[:], in_=z[:], axis=AXIS.X, op=ALU.max, negate=True)
            expz = work.tile([P, J], F32, name="expz")
            total = work.tile([P, 1], F32, name="total")
            nc.scalar.activation(
                out=expz[:].rearrange("t (u p e) -> t u p e", u=2, e=2),
                in_=z[:].rearrange("t (p u e) -> t u p e", u=2, e=2),
                func=ACT.Exp,
                bias=neg_top[:],
                accum_out=total[:],
            )
            inverse = work.tile([P, 1], F32, name="inverse")
            if i < VECTOR_INVERSES:
                nc.vector.reciprocal(out=inverse[:], in_=total[:])
            else:
                nc.gpsimd.tensor_tensor(out=inverse[:], in0=total[:], in1=minus_one[:], op=ALU.pow)
            shares[i] = (expz, inverse)

        def skip(i):
            if i < LAST:
                whole = psum.tile([P, PACK, P], F32, name="y_bank", tag="bank%d" % ((i + TILES) % (TILES + 1)))
                y_banks[i] = [(whole, range(PACK))]
            else:
                low = psum.tile([P, 2, P], F32, name="y_low", tag="bank2")
                high = psum.tile([P, 2, P], F32, name="y_high", tag="bank3")
                y_banks[i] = [(low, range(0, 2)), (high, range(2, PACK))]
            for bank, slices in y_banks[i]:
                for r in slices:
                    nc.tensor.matmul_mx(
                        out=bank[:, r - slices[0], :],
                        lhsT=ws_dealt[:, P * r : P * (r + 1)].bitcast(E4M3),
                        lhsT_scale=planes_dealt[:, P * r : P * (r + 1)],
                        rhs=xt_codes[:, 2 * P * i : 2 * P * (i + 1)].bitcast(E2M1),
                        rhs_scale=xt_plane[:, P * i : P * (i + 1)],
                        start=(r == slices[0]),
                        stop=False,
                    )

        def weigh(i):
            expz, inverse = shares[i]
            qw = work.tile([P, J], BF16, name="qw", align_bytes=64)
            nc.vector.scalar_tensor_tensor(
                out=qw[:], in0=expz[:], scalar=inverse[:], in1=fj_spread, op0=ALU.mult, op1=ALU.mult
            )
            bank = psum.tile([P, 2, P], F32, name="turn_bank", tag="turn", bufs=2)
            pairs = qw[:].bitcast(F32)
            for u in range(2):
                nc.tensor.transpose(bank[:, u, :], pairs[:, P * u : P * (u + 1)], identity[:])
            grouped = work.tile([P, PACK * P], BF16, name="grouped", align_bytes=64)
            nc.scalar.copy(
                out=grouped[:].bitcast(F32).rearrange("p (t u) -> p t u", u=2),
                in_=bank[:].rearrange("p u t -> p t u"),
            )
            turned[i] = grouped

        def rows(i):
            codes = work.tile([P, P], U32, name="codes", align_bytes=64)
            plane = work.tile([P, P], U8, name="plane", align_bytes=64)
            nc.vector.quantize_mx(out=codes[:].bitcast(E4M3), scales=plane[:], in_=turned[i][:])
            for bank, slices in y_banks[i]:
                for r in slices:
                    nc.tensor.matmul_mx(
                        out=bank[:, r - slices[0], :],
                        lhsT=wo_dealt[:, 2 * P * r : 2 * P * (r + 1)].bitcast(E2M1),
                        lhsT_scale=planes_dealt[:, N + P * r : N + P * (r + 1)],
                        rhs=codes[:].bitcast(E4M3),
                        rhs_scale=plane[:],
                        start=False,
                        stop=(r == slices[-1]),
                    )

        rounded = keep.tile([P, PACK * T], BF16, name="rounded", align_bytes=64)

        def hand_out(i):
            cols = slice(P * i, P * (i + 1))
            y = work.tile([P, PACK, P], F32, name="y")
            for bank, slices in y_banks[i]:
                nc.scalar.copy(out=y[:, slices[0] : slices[-1] + 1, :], in_=bank[:])
            nc.sync.dma_start(out=out_0.rearrange("(p r) t -> p r t", r=PACK)[:, :, cols], in_=y[:])
            nc.vector.tensor_copy(
                out=rounded[:, PACK * P * i : PACK * P * (i + 1)].rearrange("p (c a r) -> p c r a", a=4, r=PACK),
                in_=y[:].rearrange("p r (c a) -> p c r a", a=4),
            )

        def hand_out_codes(first, last):
            cols = slice(P * first, P * last)
            nc.vector.quantize_mx(
                out=y_codes[:, cols].bitcast(E4M3),
                scales=y_plane[:, cols],
                in_=rounded[:, PACK * P * first : PACK * P * last],
            )
            nc.sync.dma_start(
                out=out_1[0].rearrange("p n t -> p (n t)").bitcast(I32)[:, cols], in_=y_codes[:, cols].bitcast(I32)
            )

        for i in range(TILES):
            scores(i)
        for i in range(LAST):
            weigh(i)

        ws_dealt = keep.tile([P, N], U32, name="ws_dealt", align_bytes=64)
        nc.scalar.copy(
            out=ws_dealt[:].rearrange("p (r c a) -> p c r a", r=PACK, a=4),
            in_=ws_raw[:].bitcast(U32).rearrange("p (c a r) -> p c r a", r=PACK, a=4),
        )
        wo_dealt = keep.tile([P, 2 * N], U8, name="wo_dealt", align_bytes=64)
        nc.scalar.copy(
            out=wo_dealt[:].bitcast(U16).rearrange("p (r m) -> p r m", r=PACK),
            in_=wo_raw[:].bitcast(U16).rearrange("p (m r) -> p r m", r=PACK),
        )
        planes_dealt = keep.tile([P, 2 * N], U8, name="planes_dealt", align_bytes=64)
        for n0 in (0, N):
            nc.gpsimd.tensor_copy(
                out=planes_dealt[:, n0 : n0 + N].rearrange("p (r c a) -> p c r a", r=PACK, a=16),
                in_=w_planes[:, n0 : n0 + N].rearrange("p (c a r) -> p c r a", r=PACK, a=16),
            )

        for i in range(TILES):
            skip(i)
        rows(0)
        weigh(LAST)
        for i in range(1, TILES):
            rows(i)
        for i in range(TILES):
            hand_out(i)
        for first in range(0, TILES, 2):
            hand_out_codes(first, first + 2)
        queues = [nc.scalar, nc.scalar, nc.sync, nc.scalar]
        for quad in range(QUADS):
            partitions, scale_rows = quad_rows(quad)
            queues[quad].dma_start(out=out_2[0, scale_rows, :].bitcast(I32), in_=y_plane[partitions, :].bitcast(I32))
